import numpy as np, ml_dtypes
CORES = [2,3,42,43,82,83,122,123]
N = 8
BF = ml_dtypes.bfloat16
C, I, P, T, ST = 4096, 128, 1024, 4, 3
SX, SP = 32, 8
def parts(rng):
    return rng.integers(0, 256, (N, 8, C, 16)), rng.integers(0, 4096, (N, 8, I, 16)), rng.integers(0, 4096, (N, 8, P, 16)), rng.integers(1, 256, (N, 8, 16))
def turn(a):
    return np.ascontiguousarray(np.swapaxes(a, 2, 3)).reshape(N, 128, -1)
def pack(x, w, p, t):
    return {"xt": turn(x).astype(np.float32).astype(BF), "wd": turn(w).astype(np.int32), "pd": turn(p).astype(np.int32), "wt": np.reshape(t, (N, 128, 1)).astype(np.int32)}
def place(a, b, s):
    return ((a * b >> 5) + 37 * a + b + s) & (C - 1)
def setup_inputs(rng):
    x, w, p, t = parts(rng)
    return pack(x, w, p, t)
def setup_inputs_spread(rng):
    x, w, p, t = parts(rng)
    s = rng.choice(np.array([0.0, 0.25, 0.5, 1.0]), (N, 8, 1, 1))
    x = (x * np.exp2(-8 * s * rng.random((N, 8, C, 1)))).astype(np.int64)
    w = np.where(rng.random((N, 8, I, 1)) < 0.5, np.exp2(12 * rng.random(w.shape)).astype(np.int64) - 1, w)
    p = np.where(rng.random((N, 8, P, 1)) < 0.5, np.exp2(12 * rng.random(p.shape)).astype(np.int64) - 1, p)
    t = np.minimum(np.exp2(8 * rng.random(t.shape)).astype(np.int64), 255)
    return pack(x, np.minimum(w, 4095), np.minimum(p, 4095), t)
def setup_inputs_ends(rng):
    x, w, p, t = parts(rng); m = np.arange(16); s = np.arange(32)
    x = np.where(x < 128, 0, 255); x = np.where(rng.random(x.shape) < 0.1, np.abs(x - 1), x)
    x[:, :, (s - 1) & (C - 1)] = 0; x[:, :, (s + 37 * 4095) & (C - 1)] = 255
    w = np.where(rng.random((N, 8, I, 1)) < 0.75, 4095 * rng.integers(0, 2, w.shape), w)
    kind = rng.integers(0, 4, (N, 8, P, 1))
    p = np.where(kind == 0, 0, np.where(kind == 1, 4095, np.where(kind == 2, 4095 * rng.integers(0, 2, p.shape), p)))
    v = rng.integers(64, 2000, (N, 8))
    w[:, :, I - 1] = 0; w[:, :, I - 1, 14] = v; w[:, :, I - 1, 15] = 4095
    w[:, :, I - 2] = 4095; w[:, :, I - 2, 0] = 0; w[:, :, I - 2, 1] = v
    w[:, :, 0] = 0; w[:, :, 0, 15] = 4095; w[:, :, 1] = 4095 * (m % 2)
    p[:, :, 0] = 4095; p[:, 1::2, 0, 15] = 0
    t = np.where(t < 128, 1, 255); t[:, 0] = 1; t[:, 7] = 255
    return pack(x, w, p, t)
def setup_inputs_corners(rng):
    x, w, p, t = parts(rng); m = np.arange(16)
    kw = rng.integers(0, 6, (N, 8, I, 1)); z = rng.integers(0, 16, (N, 8, I, 1)); one = w[..., :1]
    w = np.where(kw == 0, one, np.where(kw == 1, w[..., m % 2], np.where(kw == 2, (one & 1023) + 1024 * (w & 3), np.where(kw == 3, np.where(m == z, w[..., 1:2], one), np.where(kw == 4, w[..., m % 8], w)))))
    kp = rng.integers(0, 4, (N, 8, P, 1))
    p = np.where(kp == 0, p[..., :1], np.where(kp == 1, p[..., m % 4], np.where(kp == 2, 4095 * (p & 1), p)))
    p[:, 1::2, ::SP] = w[:, 1::2]
    x[:, 0::4] = x[:, 0::4] & 1; x[:, 1::4] = x[:, 1::4][:, :, (np.arange(C) >> 2) & 7]; x[:, 2::4] = 255 * (x[:, 2::4] & 1)
    t[:, 0] = 1; t[:, 1] = 255; t[:, 2] = np.where(m == 15, 255, 1); t[:, 3] = np.where(m == 0, 1, 255)
    return pack(x, w, p, t)
def setup_inputs_crowd(rng):
    x, w, p, t = parts(rng); g1 = int(rng.integers(0, 8))
    for q in (0, 1, N - 1):
        for g in range(8):
            but = (g == g1) if q == 1 else (q > 1 and rng.random() < 0.5)
            base = rng.integers(0, 256, 16); x[q, g] = base
            if but:
                a = w[q, g]; b = np.roll(a, -1, axis=1)
                n = np.bincount(np.concatenate([place(a, b, 0).ravel(), place(b, a, 0).ravel()]), minlength=C)
                x[q, g, int(rng.choice(np.flatnonzero(n == 1)))] = 255 - base
    al = np.argsort(rng.random((8, 4096)), axis=1)[:, :4]
    a = np.take_along_axis(al, rng.integers(0, 4, (8, I)), 1)[:, :, None]; b = (a + rng.integers(1, C // 4, (8, I, 1))) & 4095
    w[2] = np.where(np.arange(16) == rng.integers(0, 16, (8, I, 1)), b, a)
    p[2, :, :, :4] = al[:, None, :]; p[2] = np.take_along_axis(p[2], np.argsort(rng.random((8, P, 16)), axis=2), 2)
    return pack(x, w, p, t)
def setup_inputs_brink(rng):
    x, w, p, t = parts(rng); m = np.arange(16)
    for q in range(N):
        for g in range(8):
            s = 1 + rng.permutation(36)
            cut = np.zeros(36, np.int64); cut[8:12] = 1
            if g % 2 == 0:
                cut[12:] = rng.integers(2, 256, 24); cut[35] = 255
            else:
                cut[12:24] = 2040; cut[24:] = 2041
            o = np.argsort(rng.random((36, 16)), axis=1)
            far = 255 - np.clip(cut[:, None] - 255 * o, 0, 255)
            lo = (255 - far) * rng.integers(0, 2, (36, 16)); up = rng.random((36, 16)) < 0.5
            x[q, g, s] = np.where(up, lo + far, lo); x[q, g, 37 * s] = np.where(up, lo, lo + far)
            p[q, g] = s[rng.integers(0, np.where(rng.random((P, 1)) < 0.5, 24, 36), (P, 16))]
            z1 = rng.integers(1, 7, (I, 1)); z2 = z1 + 2 + rng.integers(0, 8, (I, 1))
            v = np.where(m == z1, s[rng.integers(8, 12, (I, 1))], np.where(m == z2, s[rng.integers(0, 8, (I, 1))], 0))
            w[q, g] = np.where(rng.random((I, 1)) < 0.75, v, w[q, g])
    return pack(x, w, p, t)
def check_inputs(d):
    bad = []
    for k, lo, hi in (("xt", 0, 255), ("wd", 0, 4095), ("pd", 0, 4095), ("wt", 1, 255)):
        a = np.asarray(d[k]).astype(np.float64)
        if not (np.all(a >= lo) and np.all(a <= hi) and np.all(a == np.floor(a))): bad.append("range of " + k)
    return bad
def reference(xt, wd, pd, wt):
    x = np.ascontiguousarray(np.swapaxes(xt.astype(np.float32).astype(np.int32).reshape(N, 8, 16, C), 2, 3))
    w = np.ascontiguousarray(np.swapaxes(wd.astype(np.int64).reshape(N, 8, 16, I), 2, 3))
    p = np.ascontiguousarray(np.swapaxes(pd.astype(np.int64).reshape(N, 8, 16, P), 2, 3))
    wts = wt.astype(np.int64).reshape(N, 8, 1, 16)
    gi = np.arange(8)[:, None]; ti = np.arange(I)[None, :]; g3 = np.arange(8)[:, None, None]
    A = np.zeros(N, np.int64)
    for t in range(T):
        A2 = np.zeros(N, np.int64)
        for r in range(N):
            q = (r + ST * t) % N
            v = w[r].copy(); v1 = np.roll(v, -1, axis=2)
            f = x[q][g3, place(v, v1, A[q])]; h = x[q][g3, place(v1, v, A[q])]
            e = np.add.reduce(np.abs(f - h), axis=3)
            k = np.argmax(e, axis=2); kn = (k + 1) & 15
            c = np.where(e[gi, ti, (k - 1) & 15] >= e[gi, ti, kn], k, kn)
            u = np.add.reduce(wts[q] * f[gi, ti, k], axis=2)
            b = p[q][gi, u & (P - 1)]
            before = v[gi, ti, (c - 1) & 15][:, :, None]; after = v[gi, ti, (c + 1) & 15][:, :, None]
            y = x[q][g3, place(before, b, A[q])]; z = x[q][g3, place(b, after, A[q])]
            E = np.add.reduce(np.abs(y - z), axis=3)
            j = np.argmin(E, axis=2)
            good = 2 * E[gi, ti, j] < e[gi, ti, k]
            mend = v.copy(); mend[gi, ti, c] = b[gi, ti, j]
            swap = v.copy(); swap[gi, ti, k] = v[gi, ti, kn]; swap[gi, ti, kn] = v[gi, ti, k]
            new = np.where(good[:, :, None], mend, swap)
            gg, ii = np.nonzero(good)
            p[q, gg, SP * ii + (u[gg, ii] & (SP - 1))] = new[gg, ii]
            x[q, gi, SX * ti + (u & (SX - 1))] = (y[gi, ti, j] + z[gi, ti, j]) >> 1
            w[r] = new; A2[q] = (8 * I - len(gg)) & 31
        A = A2
    return {"yw": turn(w).astype(np.float32), "yp": turn(p).astype(np.float32), "yx": turn(x).astype(np.float32).astype(BF)}

import numpy as np
from concourse.mybir import AluOpType, AxisListType, ActivationFunctionType

Op = AluOpType
AF = ActivationFunctionType
NV, STEP, H = 4, 3, 2
GAM = 1.6
CH1 = [[16] * 4, [16] * 4]
CH2 = [[32] * 2, [16] * 4]
TRIES = 3000
SEED = 1
BIG = float(2 ** 24)
LAND = "la lb lc ld le".split()
EXT = {"xt": [128, 4096], "wd": [128, 128], "pd": [128, 1024], "wt": [128, 1],
       "yw": [128, 128], "yp": [128, 1024], "yx": [128, 4096]}
SCRATCH = {}
PK = {}


def bufs(where, dtype, shape, names, pack=None, halves=False):
    for n in names.split():
        for m in ([n + "0", n + "1"] if halves else [n]):
            if pack is None:
                SCRATCH[m] = (where, shape, dtype)
            else:
                o = SCRATCH[pack][1][1] if pack in SCRATCH else 0
                PK[m] = (pack, o, shape[1])
                SCRATCH[pack] = (where, [128, o + (shape[1] + 15) // 16 * 16], dtype)


bufs("sbuf", "bfloat16", [128, 4096], "rec")
bufs("sbuf", "float32", [128, 2048], "stock")
bufs("sbuf", "int32", [128, 1024], "pdi")
bufs("sbuf", "int32", [128, 128], "wdi")
bufs("sbuf", "int32", [128, 1], "wti")
bufs("sbuf", "bfloat16", [128, 2048], "K1 K2 KU")
bufs("sbuf", "bfloat16", [128, 1024], "ohJ")
bufs("sbuf", "bfloat16", [128, 64], "Tg Tx")
bufs("sbuf", "float16", [128, 4, 16], "CK1 CK2")
bufs("sbuf", "float32", [128, 4, 16], "CKc")
bufs("sbuf", "int32", [128, 4, 16], "CKi CKj")
bufs("sbuf", "int32", [128, 128], "cD cM cK cT1 cT2 cT3 tabi tabj", "PI")
bufs("sbuf", "int32", [128, 64], "oji ojk", "PI")
bufs("sbuf", "int32", [128, 8], "RC Gi Ga", "PI")
bufs("sbuf", "float32", [128, 1], "wcol Gs A32", "PF")
bufs("sbuf", "float32", [128, 128], "ISh I32", "PF")
bufs("sbuf", "float32", [128, 64], "SM2", "PF")
bufs("sbuf", "float16", [128, 128], "BO mI nI mS mP tA tB I3 I2 S3 S2 BO3 BO2 onh", "PH")
bufs("sbuf", "float16", [128, 256], "CA", "PH")
bufs("sbuf", "bfloat16", [128, 128], "BOm on16 tabe", "PB")
bufs("sbuf", "float16", [128, 64], "la lb lc ld le snd", halves=True)
bufs("sbuf", "float16", [128, 64], "bj", "PH", True)
bufs("sbuf", "float16", [128, 128], "pr", "PH", True)
bufs("sbuf", "float32", [128, 64], "M B dl Y", "PF", True)
bufs("sbuf", "float32", [128, 128], "X", "PF", True)
bufs("sbuf", "float32", [128, 4], "tf", "PF", True)
bufs("sbuf", "float32", [128, 64], "yo", halves=True)
bufs("sbuf", "int32", [128, 128], "Xi Xs", "PI", True)
bufs("sbuf", "int32", [128, 64], "hd Ms m2", "PI", True)
bufs("sbuf", "int32", [128, 16], "cc c2 ui uq sb rs FI", "PI", True)
bufs("sbuf", "uint16", [128, 128], "lu", "PU", True)
bufs("sbuf", "uint16", [128, 16], "cu uu FU", "PU", True)
bufs("sbuf", "bfloat16", [128, 128], "mk", "PB", True)
bufs("sbuf", "bfloat16", [128, 64], "mx gp nr fk", "PB", True)
bufs("sbuf", "bfloat16", [128, 4], "ng", "PB", True)
bufs("sbuf", "bfloat16", [128, 4, 256], "ab", halves=True)
bufs("sbuf", "bfloat16", [128, 1024], "f e y d", halves=True)
bufs("sbuf", "float32", [128, 4, 16], "pv cb", halves=True)
bufs("sbuf", "float32", [128, 512], "po", halves=True)
bufs("psum", "float32", [128, 512], "pA pW", halves=True)
bufs("psum", "float32", [128, 4, 128], "pE", halves=True)
A_ = slice(None)


def c(a, b, st=1):
    return slice(a, b, st)


def shift(name, s):
    o, w = PK[name][1:]
    a, b, st = s.indices(w)
    return slice(o + a, o + b, st)


def r(name, *ix, ind=None):
    if ind is not None:
        ind = (PK[ind[0]][0], shift(ind[0], ind[1]))
    if name in PK:
        return ("ref", PK[name][0], (shift(name, ix[0] if ix else A_),), ind)
    return ("ref", name, ix, ind)


def isref(x):
    return isinstance(x, tuple) and len(x) == 4 and x[0] == "ref"


def span(name, ix):
    shape = (SCRATCH[name][1] if name in SCRATCH else EXT[name])[1:]
    lo = hi = 0
    stride = 1
    for k in range(len(shape) - 1, -1, -1):
        s = ix[k] if k < len(ix) else A_
        if isinstance(s, int):
            a = b = s
        else:
            a, b, st = s.indices(shape[k])
            b = a + (b - 1 - a) // st * st
        lo += a * stride
        hi += b * stride
        stride *= shape[k]
    return lo, hi + 1


def ap(T, ref):
    x = T[ref[1]][(A_,) + tuple(ref[2])]
    return x if ref[3] is None else x.indirect(T[ref[3][0]][:, ref[3][1]])


NODES = []
ACC = {}
HALF = [""]


def add(eng, dur, calls, kind="comp", tag="", extra=(), pre=()):
    n = len(NODES)
    preds = set(pre)
    touch = list(extra)
    for m, kw in calls:
        for k, v in kw.items():
            if isref(v):
                touch.append((v[1],) + span(v[1], v[2]) + (k == "out",))
                if v[3] is not None:
                    touch.append((v[3][0],) + span(v[3][0], (v[3][1],)) + (False,))
    for name, lo, hi, w in touch:
        psum = name in SCRATCH and SCRATCH[name][0] == "psum"
        keep = []
        for q in ACC.setdefault(name, []):
            m, me, a, b, mw = q
            if m != n and psum and me != eng:
                preds.add(m)
                keep.append(q)
                continue
            if m != n and a < hi and lo < b and (w or mw):
                preds.add(m)
                if w and lo <= a and b <= hi:
                    continue
            keep.append(q)
        keep.append((n, eng, lo, hi, w))
        ACC[name] = keep
    NODES.append({"eng": eng, "dur": dur, "calls": calls, "kind": kind, "tag": tag, "preds": sorted(preds), "key": tag + HALF[0]})
    return n


def V(n, meth, tag="", **kw):
    return add("V", 25 + 1.0 * max(n, 64), [(meth, kw)], tag=tag)


def S(n, calls, tag=""):
    return add("S", sum(35 + 1.0 * max(k, 64) for k in n), [("activation", kw) for kw in calls], tag=tag)


def SG(out, win, lst, n, tag):
    return add("S", 70 + GAM * n, [("activation", dict(out=out, in_=r(win[0], *win[1:], ind=lst), func=AF.Copy))], tag=tag)


def P(calls, tag="", slow=0):
    return add("P", 60 + 40 * len(calls) + slow, [("matmul", kw) for kw in calls], tag=tag)


def I(out, pattern, base, cm, n, **kw):
    return add("G", 130 + 1.7 * n, [("iota", dict(out=out, pattern=pattern, base=base, channel_multiplier=cm, **kw))], tag="set")


def mm(out, lhsT, rhs, start=True, stop=True):
    return dict(out=out, lhsT=lhsT, rhs=rhs, start=start, stop=stop)


def ts(out, in0, s1, op0, s2=None, op1=None, n=64, tag="set"):
    kw = {} if op1 is None else {"op1": op1}
    return V(n, "tensor_scalar", tag, out=out, in0=in0, scalar1=s1, scalar2=s2, op0=op0, **kw)


def tt(out, a, b, op, n=64, tag="set"):
    return V(n, "tensor_tensor", tag, out=out, in0=a, in1=b, op=op)


def cp(out, in_, n=64, tag="set"):
    return V(n, "tensor_copy", tag, out=out, in_=in_)


def ms(out, v, n=64):
    return V(n, "memset", "set", out=out, value=v)


def scan(out, data1, tag):
    return V(64, "tensor_tensor_scan", tag, out=out, data0=r("SM2"), data1=data1, initial=BIG, op0=Op.add, op1=Op.min)


def dma(q, out, in_, dur, tag):
    return add(q, dur, [("dma_start", dict(out=out, in_=in_))], kind="dma", tag=tag)


def sums(out, K, src, first):
    return [mm(out, r("mI"), r(first), True, False)] + [
        mm(out, r(K, c(128 * k, 128 * k + 128)), r(src, A_, c(16 * k, 16 * k + 16)), False, k == 15) for k in range(16)]


def gathers(h, a, b, ta, tb, chunks):
    o = 0
    for w in chunks:
        k, e = c(16 * o, 16 * o + 16 * w), o + w
        SG(r(a + h, k), ("rec",), ("lu" + h, c(o, e)), 16 * w, ta)
        V(16 * w * GAM, "tensor_tensor", tb, out=r(b + h, k), in0=r("rec", ind=("lu" + h, c(64 + o, 64 + e))), in1=r(a + h, k), op=Op.subtract)
        S([16 * w], [dict(out=r("ab" + h, c(o // 16, e // 16), A_), in_=r(b + h, k), func=AF.Abs)], "ab" + tb)
        o = e


def build():
    AND, SAR, SLR = Op.bitwise_and, Op.arith_shift_right, Op.logical_shift_right
    dma("Y", r("wdi"), r("wd"), 2000, "load")
    dma("S", r("wti"), r("wt"), 2000, "load")
    dma("Y", r("rec", c(0, 2048)), r("xt", c(0, 2048)), 4500, "load")
    dma("S", r("rec", c(2048, 4096)), r("xt", c(2048, 4096)), 4500, "load")
    dma("Y", r("pdi"), r("pd"), 4500, "load")
    I(r("cD"), [[1, 128]], 0, -1, 128)
    I(r("cM"), [[1, 128]], 0, 0, 128)
    I(r("cK"), [[0, 128]], 0, 1, 128)
    ts(r("cT3"), r("cD"), 15, AND, n=128)
    ts(r("cT1"), r("cM"), 4, SLR, n=128)
    ts(r("cT2"), r("cK"), 4, SLR, n=128)
    tt(r("BO"), r("cT1"), r("cT2"), Op.is_equal, n=256)
    ts(r("mI"), r("cD"), 0, Op.is_equal, n=128)
    ts(r("tA"), r("cT3"), 15, Op.is_equal, n=128)
    tt(r("mS"), r("tA"), r("BO"), Op.mult, n=256)
    for o, i, k in (("I3", "mI", 3232.0), ("I2", "mI", 2080.0), ("S3", "mS", 3232.0), ("S2", "mS", 2080.0), ("nI", "mI", -1.0),
                    ("BO3", "BO", 3232.0), ("BO2", "BO", 2080.0), ("BOm", "BO", -4096.0)):
        ts(r(o), r(i), k, Op.mult)
    for h in "01":
        ts(r("la" + h), r("wdi", c(64 * int(h), 64 * int(h) + 64)), -2048.0, Op.add)
    ms(r("K1"), 0.0, 1024)
    for g in range(8):
        cp(r("K1", c(16 * g, 16 * g + 1936, 129)), r("BOm", c(16 * g, 16 * g + 16)))
    ts(r("wcol"), r("wti"), -1.0 / 2048, Op.mult)
    ts(r("KU"), r("K1"), r("wcol"), Op.mult, n=1024)
    S([2048], [dict(out=r("K2"), in_=r("K1"), func=AF.Copy, scale=-1.0)], "set")
    cp(r("I32"), r("mI"), n=128)
    ts(r("tB"), r("cT3"), 1, Op.is_equal, n=128)
    tt(r("mP"), r("tB"), r("BO"), Op.mult, n=256)
    tt(r("ISh"), r("mI"), r("mP"), Op.subtract, n=256)
    ms(r("on16"), 1.0)
    ms(r("onh"), 1.0)
    ms(r("CA", c(0, 64)), 2080.0)
    ms(r("CA", c(64, 128)), 3232.0)
    ms(r("CA", c(128, 256)), 0.0)
    I(r("CKi"), [[0, 4], [1, 16]], 0, 16, 64)
    I(r("CKc"), [[256, 4], [0, 16]], 0, 0, 64, allow_small_or_imprecise_dtypes=True)
    ts(r("CKj"), r("CKi"), 255, AND)
    tt(r("CK2"), r("CKj"), r("CKc"), Op.add, n=128)
    ts(r("CK1"), r("CK2"), 2.0, Op.mult)
    ts(r("RC", c(0, 4)), r("CK2", A_, 0), 2.0, Op.mult)
    ts(r("RC", c(4, 8)), r("CK2", A_, 0), 1.0, Op.mult)
    ms(r("SM2"), 0.0)
    ms(r("SM2", c(0, 64, 16)), BIG)
    I(r("tabi", c(0, 96)), [[1, 3], [1, 16], [1, 2]], -1, -1, 96)
    I(r("tabi", c(96, 128)), [[1, 16], [0, 2]], 0, -1, 32)
    ts(r("tabj"), r("tabi"), 15, AND, n=128)
    ts(r("tabe"), r("tabj"), 0, Op.is_equal, n=128)
    ms(r("Tg"), 0.0)
    ms(r("Tx"), 0.0)
    for o, a, x in (("Tg", 32, 0), ("Tx", 96, 1)):
        S([64], [dict(out=r(o, c(x, 64, 2)), in_=r("tabe", c(a, a + 32)), func=AF.Copy)], "set")
    I(r("oji"), [[0, 4], [1, 16]], 0, -1, 64)
    ts(r("ojk"), r("oji"), 15, AND)
    ts(r("ohJ", c(0, 64)), r("ojk"), 0, Op.is_equal)
    for k in (64, 128, 256, 512):
        S([k], [dict(out=r("ohJ", c(k, 2 * k)), in_=r("ohJ", c(0, k)), func=AF.Copy)], "set")
    for h in (0, 1):
        ts(r("stock", c(1024 * h, 1024 * h + 1024, 2)), r("pdi", c(512 * h, 512 * h + 512)), -2048.0, Op.add, n=512)
        S([512], [dict(out=r("stock", c(1024 * h + 1, 1024 * h + 1024, 2)), in_=r("stock", c(1024 * h, 1024 * h + 1024, 2)), func=AF.Copy)], "set")

    for t in range(NV):
        for hh in range(H):
            h = str(hh)
            HALF[0] = h
            al = r(LAND[t] + h)
            pA, pW, pE = "pA" + h, "pW" + h, "pE" + h
            c4, c8 = c(0, 4), c(4, 8)
            last = c(15, 64, 16)
            late = t > 0 and hh == 0
            L = [mm(r(pA, c(0, 64)), r("mS"), al)]
            if t > 0 and not late:
                L.append(mm(r(pA, c(64, 192)), r("mI"), r("CA", c(128, 256)), True, False))
            s = len(L) == 1
            L += [mm(r(pA, c(64, 128)), r("I3"), al, s, False), mm(r(pA, c(64, 128)), r("S2"), al, False, s),
                  mm(r(pA, c(128, 192)), r("I2"), al, s, False), mm(r(pA, c(128, 192)), r("S3"), al, False, True)]
            P(L, "lists")
            tt(r("M" + h), al, r(pA, c(0, 64)), Op.mult, tag="l")
            xo = "X" if late else "Xi"
            tt(r(xo + h, c(0, 64)), r("M" + h), r(pA, c(64, 128)), Op.add, tag="l")
            tt(r(xo + h, c(64, 128)), r("M" + h), r(pA, c(128, 192)), Op.add, tag="l")
            if late:
                ts(r("Xi" + h), r("X" + h), r("A32"), Op.add, n=128, tag="l2")
            ts(r("Xs" + h), r("Xi" + h), 5, SAR, 4095, AND, n=128, tag="l2")
            cp(r("lu" + h), r("Xs" + h), n=128, tag="l2")
            P([mm(r(pA, c(192, 256)), r("mI"), al), mm(r(pA, c(256, 320)), r("mI"), al),
               mm(r(pA, c(320, 384)), r("mS"), al, True, False), mm(r(pA, c(320, 384)), r("nI"), al, False, True)], "keep")
            gathers(h, "f", "e", "gf", "gd", CH1[hh])
            P(sums(r(pE, A_, c(0, 16)), "K1", "ab" + h, "CK1"), "key1")
            S([60, 4, 4], [dict(out=r("pv" + h, A_, c(1, 16)), in_=r(pE, A_, c(0, 15)), func=AF.Copy),
                           dict(out=r("pv" + h, A_, 0), in_=r(pE, A_, 15), func=AF.Copy, bias=-32.0),
                           dict(out=r(pE, A_, 16), in_=r(pE, A_, 0), func=AF.Copy, bias=32.0)], "ring")
            tt(r("cb" + h), r("pv" + h), r(pE, A_, c(1, 17)), Op.is_gt, tag="a")
            tt(r(pW, c(384, 448)), r("cb" + h), r(pE, A_, c(0, 16)), Op.add, tag="a")
            scan(r("Ms" + h), r(pW, c(384, 448)), "a")
            ts(r("cc" + h, c8), r("Ms" + h, last), 1, SAR, 1023, AND, tag="a")
            ts(r("cc" + h, c4), r("Ms" + h, last), 31, AND, tag="a")
            cp(r("cu" + h, c(0, 8)), r("cc" + h, c(0, 8)), tag="a2")
            SG(r("fk" + h), ("f" + h,), ("cu" + h, c8), 64, "fk")
            P([mm(r(pE, 0, c(64, 68)), r("KU", c(128 * k, 128 * k + 128)), r("fk" + h, c(k, 64, 16)), k == 0, k == 15) for k in range(16)], "u")
            for k in (0, 64):
                SG(r("mk" + h, c(k, k + 64)), ("tabe", c(k, k + 32)), ("cu" + h, c4), 64, "mask")
            tt(r("pr" + h), r("mk" + h), r(pA, c(192, 320)), Op.mult, n=128, tag="a3")
            P([mm(r(pW, c(0, 256)), r("mI"), r("CA"), True, False), mm(r(pW, c(0, 128)), r("BO"), r("pr" + h), False, False),
               mm(r(pW, c(128, 192)), r("BO3"), r("pr" + h, c(0, 64)), False, False),
               mm(r(pW, c(192, 256)), r("BO2"), r("pr" + h, c(64, 128)), False, True)], "wl", 100)
            cp(r("ui" + h, c4), r(pE, 0, c(64, 68)), tag="o")
            ts(r("uq" + h, c4), r("ui" + h, c4), 2046, AND, tag="o")
            cp(r("uu" + h, c4), r("uq" + h, c4), tag="o")
            SG(r("B" + h), ("stock",), ("uu" + h, c4), 64, "B")
            tt(r("X" + h, c(0, 64)), r("B" + h), r(pW, c(0, 64)), Op.mult, tag="m")
            tt(r("X" + h, c(64, 128)), r("B" + h), r(pW, c(64, 128)), Op.mult, tag="m")
            tt(r("Xi" + h), r("X" + h), r(pW, c(128, 256)), Op.add, n=128, tag="m")
            ts(r("Xs" + h), r("Xi" + h), 5, SAR, 4095, AND, n=128, tag="m")
            cp(r("lu" + h), r("Xs" + h), n=128, tag="m")
            gathers(h, "y", "d", "gy", "gz", CH2[hh])
            P(sums(r(pW, c(448, 512)), "K2", "ab" + h, "CK2"), "key2")
            ts(r("tf" + h), r("Ms" + h, last), -0.5, Op.mult, tag="pre")
            ts(r("c2" + h, c4), r("cc" + h, c4), 2.0, Op.mult, tag="pre")
            ts(r("rs" + h, c4), r("ui" + h, c4), 1, SAR, 31, AND, tag="pre")
            ts(r("rs" + h, c8), r("ui" + h, c4), 14, AND, tag="pre")
            tt(r("FI" + h, c8), r("rs" + h, c4), r("RC", c4), Op.add, tag="pre")
            tt(r("sb" + h, c4), r("rs" + h, c8), r("RC", c8), Op.add, tag="pre")
            scan(r("m2" + h), r(pW, c(448, 512)), "b")
            tt(r("ng" + h), r("m2" + h, last), r("tf" + h), Op.is_ge, tag="b")
            ts(r("FI" + h, c4), r("m2" + h, last), 1023, AND, tag="b")
            tt(r("FI" + h, c(12, 16)), r("c2" + h, c4), r("ng" + h), Op.add, tag="b")
            tt(r("FI" + h, c(8, 12)), r("sb" + h, c4), r("ng" + h), Op.add, tag="b")
            cp(r("FU" + h), r("FI" + h), tag="b2")
            SG(r("mx" + h), ("Tx",), ("FU" + h, c(12, 16)), 64, "mask2")
            SG(r("gp" + h), ("Tg",), ("FU" + h, c(12, 16)), 64, "mask2")
            V(150, "tensor_tensor", "w", out=r("bj" + h), in0=r("ohJ", ind=("FU" + h, c4)), in1=r("B" + h), op=Op.mult)
            P([mm(r(pW, c(256, 320)), r("BO"), r("bj" + h), True, False), mm(r(pW, c(256, 320)), r("nI"), al, False, True)], "bj")
            tt(r("dl" + h), r("mx" + h), r(pA, c(320, 384)), Op.mult, tag="w")
            P([mm(r(pW, c(320, 384)), r("mI"), al, True, False), mm(r(pW, c(320, 384)), r("ISh"), r("dl" + h), False, True)], "R", 150)
            tt(r("Y" + h), r("gp" + h), r(pW, c(256, 320)), Op.mult, tag="w")
            tt(r("snd" + h), r("Y" + h), r(pW, c(320, 384)), Op.add, tag="w")
            sn = add("G", 300, [("remote_dma", dict(to=LAND[t + 1] + h, in_=r("snd" + h)))], kind="send", tag="%d%d" % (t, hh))
            add("R", 2300, [], kind="recv", tag="%d%d" % (t, hh), pre=[sn], extra=[(LAND[t + 1] + h, 0, 64, True)])
            V(150, "tensor_scalar", "nr", out=r("hd" + h), in0=r("d" + h, ind=("FU" + h, c4)), scalar1=0.5, scalar2=-0.25, op0=Op.mult, op1=Op.add)
            V(150, "tensor_tensor", "nr", out=r("nr" + h), in0=r("y" + h, ind=("FU" + h, c4)), in1=r("hd" + h), op=Op.add)
        for hh in range(H):
            h = HALF[0] = str(hh)
            V(240, "tensor_copy", "sr", out=r("rec", c(2048 * hh, 2048 * hh + 2048), ind=("FU" + h, c(4, 8))), in_=r("nr" + h))
        HALF[0] = ""
        if t + 1 < NV:
            pa = r("pE1", 0, c(116, 120))
            P([mm(pa, r("on16"), r("ng0"), True, False), mm(pa, r("on16"), r("ng1"), False, True)], "A")
            V(64, "tensor_reduce", "A", out=r("Gs"), in_=pa, axis=AxisListType.X, op=Op.add)
            cp(r("Gi", c(0, 1)), r("Gs"), tag="A")
            ts(r("Ga", c(0, 1)), r("Gi", c(0, 1)), 31, AND, tag="A")
            ts(r("A32"), r("Ga", c(0, 1)), 32.0, Op.mult, tag="A")
            ts(r("CA", c(128, 256)), r("onh"), r("A32"), Op.mult, n=128, tag="CA")
        for hh in range(H):
            h = HALF[0] = str(hh)
            V(240, "tensor_copy", "ss", out=r("stock", c(1024 * hh, 1024 * hh + 1024), ind=("FU" + h, c(8, 12))), in_=r("snd" + h))
    for hh in range(H):
        h = HALF[0] = str(hh)
        dma("Y", r("yx", c(2048 * hh, 2048 * hh + 2048)), r("rec", c(2048 * hh, 2048 * hh + 2048)), 3000, "store")
        S([512], [dict(out=r("po" + h), in_=r("stock", c(1024 * hh, 1024 * hh + 1024, 2)), func=AF.Copy, bias=2048.0)], "po")
        dma("Y", r("yp", c(512 * hh, 512 * hh + 512)), r("po" + h), 2500, "store")
        ts(r("yo" + h), r("le" + h), 2048.0, Op.add, tag="yo")
        dma("Y", r("yw", c(64 * hh, 64 * hh + 64)), r("yo" + h), 2000, "store")


def ways():
    n = len(NODES)
    succ = [[] for _ in range(n)]
    for i, x in enumerate(NODES):
        for p in x["preds"]:
            succ[p].append(i)
    way = [0.0] * n
    for i in range(n - 1, -1, -1):
        way[i] = NODES[i]["dur"] + max([way[j] + 110.0 for j in succ[i]], default=0.0)
    return succ, way


def schedule(bonus, sw):
    succ, way = sw
    n = len(NODES)
    prio = [way[i] + bonus.get(NODES[i]["key"], 0) for i in range(n)]
    look = {q: bonus.get("look" + q, 0) for q in "VSPGYR"}
    left = [len(x["preds"]) for x in NODES]
    rt = [0.0] * n
    ready = {}
    for i in range(n):
        if left[i] == 0:
            ready.setdefault(NODES[i]["eng"], []).append(i)
    free = {}
    order = []
    end = 0.0
    while len(order) < n:
        s, e = min((max(free.get(q, 0.0), min(rt[i] for i in L)), q) for q, L in ready.items() if L)
        i = max((i for i in ready[e] if rt[i] <= s + look[e]), key=lambda k: (prio[k] - 10 * max(rt[k] - s, 0), -k))
        s = max(s, rt[i])
        ready[e].remove(i)
        x = NODES[i]
        free[e] = s + (100.0 if x["kind"] == "dma" else 0.0 if x["kind"] == "recv" else x["dur"])
        x["t0"], x["t1"] = s, s + x["dur"]
        end = max(end, x["t1"])
        order.append(i)
        for j in succ[i]:
            left[j] -= 1
            rt[j] = max(rt[j], x["t1"] + (60.0 if NODES[j]["eng"] == e else 110.0))
            if left[j] == 0:
                ready.setdefault(NODES[j]["eng"], []).append(j)
    return order, end


def search(tries, seed):
    rnd = np.random.RandomState(seed)
    sw = ways()
    keys = sorted({x["key"] for x in NODES})
    B = {q: 1500 for q in keys if q.endswith("0") and q[0] != "s"}
    B.update({"A": 6000, "sr0": 5000, "sr1": 5000, "ss0": -9000, "ss1": -9000, "set": -3000, "lookS": 50, "lookV": 100})
    best, end = schedule(B, sw)
    steps = (-8000, -4000, -2000, -1000, -500, 500, 1000, 2000, 4000, 8000)
    for _ in range(tries):
        C = dict(B)
        for _ in range((1, 1, 2, 3, 6)[rnd.randint(5)]):
            k = rnd.randint(len(keys) + 6)
            if k >= len(keys):
                C["look" + "VSP"[k % 3]] = (0, 50, 100, 200, 300, 500)[rnd.randint(6)]
            else:
                C[keys[k]] = steps[rnd.randint(10)] + (C.get(keys[k], 0) if rnd.randint(2) else 0)
        o, v = schedule(C, sw)
        if v <= end:
            best, end, B = o, v, C
    return schedule(B, sw)[0]


def plan(order):
    cnt, know, comp, out, final = {}, {}, {}, [], {}
    for i in order:
        x = NODES[i]
        e, kind = x["eng"], x["kind"]
        K = know.setdefault(e, {})
        waits = []
        need = {}
        for p in (x["preds"] if kind != "recv" else []):
            sm, v = NODES[p]["tok"]
            if need.get(sm, (0, 0))[0] < v:
                need[sm] = (v, p)
        for sm, (v, p) in sorted(need.items(), key=lambda z: -NODES[z[1][1]]["t1"]):
            if K.get(sm, 0) < v:
                waits.append((sm, v))
                for a, b in NODES[p]["clk"].items():
                    K[a] = max(K.get(a, 0), b)
        clk = dict(K) if kind != "recv" else {}
        if kind == "comp":
            sm = "s" + e
            v = cnt[sm] = cnt.get(sm, 0) + (1 if x["calls"][0][0] == "matmul" else len(x["calls"]))
            for a, b in comp.get(e, {}).items():
                clk[a] = max(clk.get(a, 0), b)
            comp[e] = clk
        elif kind == "dma":
            sm, v = "d%d" % i, 16
        else:
            sm, v = ("l" if kind == "send" else "r") + x["tag"], 8
        clk[sm] = v
        x["tok"], x["clk"] = (sm, v), clk
        final[sm] = v
        out.append((i, waits))
    return out, final, know["G"]


build()
PLAN, FINAL, KNOWG = plan(search(TRIES, SEED))
SEMAPHORES = list(FINAL)


def rank_program(g, core, T, topo):
    rank = T.rank_of(core)
    if rank is None:
        return
    n = len(T.cores)
    Q = {"V": g.vector, "S": g.scalar, "P": g.tensor, "G": g, "Y": g.sync}
    for i, waits in PLAN:
        x = NODES[i]
        if x["kind"] == "recv":
            continue
        q = Q[x["eng"]]
        for sm, v in waits:
            q.wait_ge(T.sem[sm], v)
        if x["kind"] == "send":
            t = int(x["tag"][0])
            dst = T.cores[(rank + (STEP if t + 1 < NV else -STEP * (NV - 1))) % n]
            kw = x["calls"][0][1]
            rid, pid = topo.addr(dst)[:2]
            g.remote_dma(out_ap=T[kw["to"]][:], in_ap=ap(T, kw["in_"]), remote_sem=T.sem["r" + x["tag"]], local_sem=T.sem["l" + x["tag"]],
                         pid=pid, routing_id=rid, dma_engine_mask=sum(1 << e for e in topo.engines(core, dst)[:8]))
            continue
        k = len(x["calls"])
        for m, kw in x["calls"]:
            k -= 1
            kw = {a: (ap(T, b) if isref(b) else b) for a, b in kw.items()}
            if m == "memset":
                ins = q.memset(kw["out"], kw["value"])
            elif m == "dma_start":
                ins = q.dma_start(kw["out"], kw["in_"])
            elif m == "matmul":
                ins = q.matmul(kw["out"], kw["lhsT"], kw["rhs"], kw["start"], kw["stop"])
            elif m == "iota":
                ins = q.iota(kw.pop("out"), **kw)
            elif m == "activation":
                ins = q.activation(**kw)
            else:
                ins = {"tensor_copy": q.tensor_copy, "tensor_tensor": q.tensor_tensor, "tensor_scalar": q.tensor_scalar,
                       "tensor_reduce": q.tensor_reduce, "tensor_tensor_scan": q.tensor_tensor_scan}[m](**kw)
            if x["kind"] == "dma":
                ins.then_inc(T.sem[x["tok"][0]], 16)
            elif m != "matmul" or k == 0:
                ins.then_inc(T.sem[x["tok"][0]], 1)
    for sm in SEMAPHORES:
        if KNOWG.get(sm, 0) < FINAL[sm]:
            g.wait_ge(T.sem[sm], FINAL[sm])
